import numpy as np
import ml_dtypes

BF16 = ml_dtypes.bfloat16


def bf(x):
    return np.asarray(x, np.float32).astype(BF16)


def f32(x):
    return np.asarray(x, np.float32)


def f64(x):
    return np.asarray(x).astype(np.float64)


def striped(idx):
    return np.tile(idx.reshape(-1, 16).T, (8, 1))


S, K, M, N, D, V = 2048, 512, 128, 768, 4, 192


def gelu_tanh(v):
    return 0.5 * v * (1.0 + np.tanh(np.sqrt(2.0 / np.pi) * (v + 0.044715 * v**3)))


def setup_inputs():
    return {"table": bf(np.random.standard_normal((K, S))), "w": bf(np.random.standard_normal((K, M)) / np.sqrt(K)), "b": f32(0.5 * np.random.standard_normal((M, 1))), "offs": striped(np.random.permutation(np.tile(np.arange(S), 2))[:N])}


def reference(table, w, b, offs):
    idx = offs[:16].T.reshape(-1)
    x = f64(table)[:, idx]
    y = f64(w).T @ x
    z = gelu_tanh(y + f64(b))
    return z.reshape(M, V, D).mean(axis=2)

@@ -1,0 +1,62 @@
+import concourse.mybir as mybir
+
+BF16, F32, U16 = mybir.dt.bfloat16, mybir.dt.float32, mybir.dt.uint16
+
+P = 128
+K, S = 512, 2048
+M = 128
+N = 768
+GROUP = 4
+K_BLOCKS = K // P
+PIECE = 384
+PIECES = N // PIECE
+PIECE_OFFSET_COLUMNS = PIECE // 16
+PIECE_NODES = PIECE // GROUP
+
+FLOPS = 2 * K * M * N
+BYTES = N * K * 2 + K * M * 2 + M * 4 + N * 2 + M * (N // GROUP) * 4
+
+
+def tile_gather_matmul_kernel(tc, table, w, b, offs, out):
+    nc = tc.nc
+    with (
+        tc.tile_pool(name="held", bufs=1) as held,
+        tc.psum_pool(name="psum", bufs=1) as psum,
+    ):
+        offsets = held.tile([P, N // 16], U16, name="offsets")
+        nc.sync.dma_start(offsets[:], offs)
+        weights = held.tile([P, K_BLOCKS, M], BF16, name="weights")
+        nc.scalar.dma_start(weights[:], w.rearrange("(a p) m -> p a m", p=P))
+        bias = held.tile([P, 1], F32, name="bias")
+        nc.scalar.dma_start(bias[:], b)
+        blocks = []
+        for a in range(K_BLOCKS):
+            block = held.tile([P, S], BF16, name=f"block{a}")
+            nc.sync.dma_start(block[:], table[a * P : (a + 1) * P, :])
+            blocks.append(block)
+
+        banks = [psum.tile([P, PIECE], F32, name=f"bank{i}") for i in range(PIECES)]
+        for a in range(K_BLOCKS):
+            for i in range(PIECES):
+                piece_offsets = offsets[:, i * PIECE_OFFSET_COLUMNS : (i + 1) * PIECE_OFFSET_COLUMNS]
+                nc.tensor.matmul(
+                    banks[i][:],
+                    weights[:, a, :],
+                    blocks[a][:].indirect(piece_offsets),
+                    start=(a == 0),
+                    stop=(a == K_BLOCKS - 1),
+                )
+
+        for i in range(PIECES):
+            activated = held.tile([P, PIECE_NODES, GROUP], F32, name=f"activated{i}")
+            nc.scalar.activation(
+                activated[:].rearrange("p v t -> p (v t)"),
+                banks[i][:],
+                mybir.ActivationFunctionType.Gelu_apprx_tanh,
+                bias=bias[:, 0:1],
+            )
+            sums = held.tile([P, PIECE_NODES], F32, name=f"sums{i}")
+            nc.vector.tensor_reduce(sums[:], activated[:], axis=mybir.AxisListType.X, op=mybir.AluOpType.add)
+            means = held.tile([P, PIECE_NODES], F32, name=f"means{i}")
+            nc.vector.tensor_scalar_mul(means[:], sums[:], 1.0 / GROUP)
+            nc.sync.dma_start(out[:, i * PIECE_NODES : (i + 1) * PIECE_NODES], means[:])

@@ -8,10 +8,11 @@ M = 128
 N = 768
 GROUP = 4
 K_BLOCKS = K // P
-PIECE = 384
+PIECE = 256
 PIECES = N // PIECE
 PIECE_OFFSET_COLUMNS = PIECE // 16
 PIECE_NODES = PIECE // GROUP
+WARM_UP_MATMULS = 6
 
 FLOPS = 2 * K * M * N
 BYTES = N * K * 2 + K * M * 2 + M * 4 + N * 2 + M * (N // GROUP) * 4
@@ -26,14 +27,21 @@ def tile_gather_matmul_kernel(tc, table, w, b, offs, out):
         offsets = held.tile([P, N // 16], U16, name="offsets")
         nc.sync.dma_start(offsets[:], offs)
         weights = held.tile([P, K_BLOCKS, M], BF16, name="weights")
-        nc.scalar.dma_start(weights[:], w.rearrange("(a p) m -> p a m", p=P))
+        nc.scalar.dma_start(weights[:], w.rearrange("(p a) m -> p a m", a=K_BLOCKS))
         bias = held.tile([P, 1], F32, name="bias")
         nc.scalar.dma_start(bias[:], b)
+        table_blocks = table.rearrange("(p a) s -> a p s", a=K_BLOCKS)
         blocks = []
         for a in range(K_BLOCKS):
             block = held.tile([P, S], BF16, name=f"block{a}")
-            nc.sync.dma_start(block[:], table[a * P : (a + 1) * P, :])
+            nc.sync.dma_start(block[:], table_blocks[a])
             blocks.append(block)
+
+        zeros = held.tile([P, 512], BF16, name="zeros")
+        nc.vector.memset(zeros[:], 0.0)
+        unused = psum.tile([P, 512], F32, name="unused")
+        for _ in range(WARM_UP_MATMULS):
+            nc.tensor.matmul(unused[:], zeros[:, 0:P], zeros[:], start=True, stop=True)
 
         banks = [psum.tile([P, PIECE], F32, name=f"bank{i}") for i in range(PIECES)]
         for a in range(K_BLOCKS):

@@ -12,7 +12,7 @@ PIECE = 256
 PIECES = N // PIECE
 PIECE_OFFSET_COLUMNS = PIECE // 16
 PIECE_NODES = PIECE // GROUP
-WARM_UP_MATMULS = 6
+NODES = N // GROUP
 
 FLOPS = 2 * K * M * N
 BYTES = N * K * 2 + K * M * 2 + M * 4 + N * 2 + M * (N // GROUP) * 4
@@ -37,12 +37,6 @@ def tile_gather_matmul_kernel(tc, table, w, b, offs, out):
             nc.sync.dma_start(block[:], table_blocks[a])
             blocks.append(block)
 
-        zeros = held.tile([P, 512], BF16, name="zeros")
-        nc.vector.memset(zeros[:], 0.0)
-        unused = psum.tile([P, 512], F32, name="unused")
-        for _ in range(WARM_UP_MATMULS):
-            nc.tensor.matmul(unused[:], zeros[:, 0:P], zeros[:], start=True, stop=True)
-
         banks = [psum.tile([P, PIECE], F32, name=f"bank{i}") for i in range(PIECES)]
         for a in range(K_BLOCKS):
             for i in range(PIECES):
@@ -55,6 +49,7 @@ def tile_gather_matmul_kernel(tc, table, w, b, offs, out):
                     stop=(a == K_BLOCKS - 1),
                 )
 
+        sums = held.tile([P, NODES], F32, name="sums")
         for i in range(PIECES):
             activated = held.tile([P, PIECE_NODES, GROUP], F32, name=f"activated{i}")
             nc.scalar.activation(
@@ -63,8 +58,12 @@ def tile_gather_matmul_kernel(tc, table, w, b, offs, out):
                 mybir.ActivationFunctionType.Gelu_apprx_tanh,
                 bias=bias[:, 0:1],
             )
-            sums = held.tile([P, PIECE_NODES], F32, name=f"sums{i}")
-            nc.vector.tensor_reduce(sums[:], activated[:], axis=mybir.AxisListType.X, op=mybir.AluOpType.add)
-            means = held.tile([P, PIECE_NODES], F32, name=f"means{i}")
-            nc.vector.tensor_scalar_mul(means[:], sums[:], 1.0 / GROUP)
-            nc.sync.dma_start(out[:, i * PIECE_NODES : (i + 1) * PIECE_NODES], means[:])
+            nc.vector.tensor_reduce(
+                sums[:, i * PIECE_NODES : (i + 1) * PIECE_NODES],
+                activated[:],
+                axis=mybir.AxisListType.X,
+                op=mybir.AluOpType.add,
+            )
+        means = held.tile([P, NODES], F32, name="means")
+        nc.vector.tensor_scalar_mul(means[:], sums[:], 1.0 / GROUP)
+        nc.sync.dma_start(out, means[:])

@@ -13,6 +13,7 @@ PIECES = N // PIECE
 PIECE_OFFSET_COLUMNS = PIECE // 16
 PIECE_NODES = PIECE // GROUP
 NODES = N // GROUP
+EARLY_NODES = NODES - PIECE_NODES
 
 FLOPS = 2 * K * M * N
 BYTES = N * K * 2 + K * M * 2 + M * 4 + N * 2 + M * (N // GROUP) * 4
@@ -65,5 +66,6 @@ def tile_gather_matmul_kernel(tc, table, w, b, offs, out):
                 op=mybir.AluOpType.add,
             )
         means = held.tile([P, NODES], F32, name="means")
-        nc.vector.tensor_scalar_mul(means[:], sums[:], 1.0 / GROUP)
-        nc.sync.dma_start(out, means[:])
+        for first, last in ((0, EARLY_NODES), (EARLY_NODES, NODES)):
+            nc.vector.tensor_scalar_mul(means[:, first:last], sums[:, first:last], 1.0 / GROUP)
+            nc.sync.dma_start(out[:, first:last], means[:, first:last])

@@ -68,4 +68,4 @@ def tile_gather_matmul_kernel(tc, table, w, b, offs, out):
         means = held.tile([P, NODES], F32, name="means")
         for first, last in ((0, EARLY_NODES), (EARLY_NODES, NODES)):
             nc.vector.tensor_scalar_mul(means[:, first:last], sums[:, first:last], 1.0 / GROUP)
-            nc.sync.dma_start(out[:, first:last], means[:, first:last])
+        nc.sync.dma_start(out, means[:])

@@ -14,6 +14,8 @@ PIECE_OFFSET_COLUMNS = PIECE // 16
 PIECE_NODES = PIECE // GROUP
 NODES = N // GROUP
 EARLY_NODES = NODES - PIECE_NODES
+SCALAR_NODES = PIECE_NODES // 4
+VECTOR_NODES = NODES - SCALAR_NODES
 
 FLOPS = 2 * K * M * N
 BYTES = N * K * 2 + K * M * 2 + M * 4 + N * 2 + M * (N // GROUP) * 4
@@ -50,7 +52,8 @@ def tile_gather_matmul_kernel(tc, table, w, b, offs, out):
                     stop=(a == K_BLOCKS - 1),
                 )
 
-        sums = held.tile([P, NODES], F32, name="sums")
+        sums = held.tile([P, VECTOR_NODES], F32, name="sums")
+        means = held.tile([P, NODES], F32, name="means")
         for i in range(PIECES):
             activated = held.tile([P, PIECE_NODES, GROUP], F32, name=f"activated{i}")
             nc.scalar.activation(
@@ -59,13 +62,18 @@ def tile_gather_matmul_kernel(tc, table, w, b, offs, out):
                 mybir.ActivationFunctionType.Gelu_apprx_tanh,
                 bias=bias[:, 0:1],
             )
+            summed_here = min((i + 1) * PIECE_NODES, VECTOR_NODES) - i * PIECE_NODES
             nc.vector.tensor_reduce(
-                sums[:, i * PIECE_NODES : (i + 1) * PIECE_NODES],
-                activated[:],
+                sums[:, i * PIECE_NODES : i * PIECE_NODES + summed_here],
+                activated[:, 0:summed_here, :],
                 axis=mybir.AxisListType.X,
                 op=mybir.AluOpType.add,
             )
-        means = held.tile([P, NODES], F32, name="means")
-        for first, last in ((0, EARLY_NODES), (EARLY_NODES, NODES)):
+        quartered = held.tile([P, SCALAR_NODES, GROUP], F32, name="quartered")
+        nc.scalar.mul(quartered[:], activated[:, PIECE_NODES - SCALAR_NODES : PIECE_NODES, :], 1.0 / GROUP)
+        nc.vector.tensor_reduce(
+            means[:, VECTOR_NODES:NODES], quartered[:], axis=mybir.AxisListType.X, op=mybir.AluOpType.add
+        )
+        for first, last in ((0, EARLY_NODES), (EARLY_NODES, VECTOR_NODES)):
             nc.vector.tensor_scalar_mul(means[:, first:last], sums[:, first:last], 1.0 / GROUP)
         nc.sync.dma_start(out, means[:])

@@ -52,6 +52,15 @@ def tile_gather_matmul_kernel(tc, table, w, b, offs, out):
                     stop=(a == K_BLOCKS - 1),
                 )
 
+        wake_activated = held.tile([P, 1, GROUP], F32, name="wake_activated")
+        nc.scalar.activation(
+            wake_activated[:].rearrange("p v t -> p (v t)"),
+            blocks[K_BLOCKS - 2][:, 0:GROUP],
+            mybir.ActivationFunctionType.Gelu_apprx_tanh,
+        )
+        wake_sum = held.tile([P, 1], F32, name="wake_sum")
+        nc.vector.tensor_reduce(wake_sum[:], wake_activated[:], axis=mybir.AxisListType.X, op=mybir.AluOpType.add)
+
         sums = held.tile([P, VECTOR_NODES], F32, name="sums")
         means = held.tile([P, NODES], F32, name="means")
         for i in range(PIECES):

import concourse.mybir as mybir

BF16, F32, U16 = mybir.dt.bfloat16, mybir.dt.float32, mybir.dt.uint16

P = 128
K, S = 512, 2048
M = 128
N = 768
GROUP = 4
K_BLOCKS = K // P
PIECE = 256
PIECES = N // PIECE
PIECE_OFFSET_COLUMNS = PIECE // 16
PIECE_NODES = PIECE // GROUP
NODES = N // GROUP
EARLY_NODES = NODES - PIECE_NODES
SCALAR_NODES = PIECE_NODES // 4
VECTOR_NODES = NODES - SCALAR_NODES

FLOPS = 2 * K * M * N
BYTES = N * K * 2 + K * M * 2 + M * 4 + N * 2 + M * (N // GROUP) * 4


def tile_gather_matmul_kernel(tc, table, w, b, offs, out):
    nc = tc.nc
    with (
        tc.tile_pool(name="held", bufs=1) as held,
        tc.psum_pool(name="psum", bufs=1) as psum,
    ):
        offsets = held.tile([P, N // 16], U16, name="offsets")
        nc.sync.dma_start(offsets[:], offs)
        weights = held.tile([P, K_BLOCKS, M], BF16, name="weights")
        nc.scalar.dma_start(weights[:], w.rearrange("(p a) m -> p a m", a=K_BLOCKS))
        bias = held.tile([P, 1], F32, name="bias")
        nc.scalar.dma_start(bias[:], b)
        table_blocks = table.rearrange("(p a) s -> a p s", a=K_BLOCKS)
        blocks = []
        for a in range(K_BLOCKS):
            block = held.tile([P, S], BF16, name=f"block{a}")
            nc.sync.dma_start(block[:], table_blocks[a])
            blocks.append(block)

        banks = [psum.tile([P, PIECE], F32, name=f"bank{i}") for i in range(PIECES)]
        for a in range(K_BLOCKS):
            for i in range(PIECES):
                piece_offsets = offsets[:, i * PIECE_OFFSET_COLUMNS : (i + 1) * PIECE_OFFSET_COLUMNS]
                nc.tensor.matmul(
                    banks[i][:],
                    weights[:, a, :],
                    blocks[a][:].indirect(piece_offsets),
                    start=(a == 0),
                    stop=(a == K_BLOCKS - 1),
                )

        wake_activated = held.tile([P, 1, GROUP], F32, name="wake_activated")
        nc.scalar.activation(
            wake_activated[:].rearrange("p v t -> p (v t)"),
            blocks[K_BLOCKS - 2][:, 0:GROUP],
            mybir.ActivationFunctionType.Gelu_apprx_tanh,
        )
        wake_sum = held.tile([P, 1], F32, name="wake_sum")
        nc.vector.tensor_reduce(wake_sum[:], wake_activated[:], axis=mybir.AxisListType.X, op=mybir.AluOpType.add)

        sums = held.tile([P, VECTOR_NODES], F32, name="sums")
        means = held.tile([P, NODES], F32, name="means")
        for i in range(PIECES):
            activated = held.tile([P, PIECE_NODES, GROUP], F32, name=f"activated{i}")
            nc.scalar.activation(
                activated[:].rearrange("p v t -> p (v t)"),
                banks[i][:],
                mybir.ActivationFunctionType.Gelu_apprx_tanh,
                bias=bias[:, 0:1],
            )
            summed_here = min((i + 1) * PIECE_NODES, VECTOR_NODES) - i * PIECE_NODES
            nc.vector.tensor_reduce(
                sums[:, i * PIECE_NODES : i * PIECE_NODES + summed_here],
                activated[:, 0:summed_here, :],
                axis=mybir.AxisListType.X,
                op=mybir.AluOpType.add,
            )
        quartered = held.tile([P, SCALAR_NODES, GROUP], F32, name="quartered")
        nc.scalar.mul(quartered[:], activated[:, PIECE_NODES - SCALAR_NODES : PIECE_NODES, :], 1.0 / GROUP)
        nc.vector.tensor_reduce(
            means[:, VECTOR_NODES:NODES], quartered[:], axis=mybir.AxisListType.X, op=mybir.AluOpType.add
        )
        for first, last in ((0, EARLY_NODES), (EARLY_NODES, VECTOR_NODES)):
            nc.vector.tensor_scalar_mul(means[:, first:last], sums[:, first:last], 1.0 / GROUP)
        nc.sync.dma_start(out, means[:])
